import numpy as np
import ml_dtypes


def mxq(x, axis, fmt="e4m3"):
    dtype, down = {"e4m3": (ml_dtypes.float8_e4m3fn, 7), "e5m2": (ml_dtypes.float8_e5m2, 14)}[fmt]
    v = np.moveaxis(np.asarray(x, np.float32).astype(ml_dtypes.bfloat16).astype(np.float64), axis, -1)
    blocks = v.reshape(v.shape[:-1] + (-1, 32))
    amax = np.abs(blocks).max(-1, keepdims=True)
    byte = np.maximum(np.where(amax > 0, np.frexp(amax)[1] - 1 + 127, 0) - down, 1)
    scale = np.exp2(byte - 127.0)
    codes = (blocks / scale).astype(np.float32).astype(dtype).astype(np.float64)
    return np.moveaxis((codes * scale).reshape(v.shape), -1, axis)


WIDE = False


def mx_kscale(k):
    if not WIDE:
        return np.ones(k)
    levels = np.array([10, -10, 5, -5, 0])
    if k % 512:
        return np.exp2(np.random.permutation(np.resize(levels, k // 32))).repeat(32)
    a = np.empty((k // 512, 16))
    for p in range(k // 512):
        a[p, :8] = np.random.permutation(np.resize(levels, 8))
        for g in range(8):
            far = levels[np.abs(levels - a[p, g]) >= 10]
            a[p, g + 8] = far[np.random.randint(len(far))]
    return np.exp2(a.ravel()).repeat(32)


def f64(x):
    return np.asarray(x).astype(np.float64)


def striped(idx):
    return np.tile(np.asarray(idx).reshape(-1, 16).T, (8, 1)).astype(np.uint16)


def unstriped(offs):
    return offs[:16].T.reshape(-1).astype(np.int64)


E2M1 = np.array([0.0, 0.5, 1.0, 1.5, 2.0, 3.0, 4.0, 6.0, -0.0, -0.5, -1.0, -1.5, -2.0, -3.0, -4.0, -6.0])


def pack_weight(w, fmt):
    k, n = w.shape
    w = f64(np.asarray(w, np.float32).astype(ml_dtypes.bfloat16)).reshape(k // 32, 32, n)
    amax = np.abs(w).max(1)
    if fmt == "e4m3":
        byte = np.frexp(amax)[1] - 1 + 127 - 7
    else:
        mant, ex = np.frexp(amax / 6.0)
        byte = np.where(mant > 0.5, ex, ex - 1) + 127
    byte = np.clip(np.where(amax > 0, byte, 1), 1, 254)
    scaled = (w * np.exp2(127.0 - byte)[:, None, :]).reshape(k, n).astype(np.float32)
    by_word = np.ascontiguousarray(scaled.reshape(k // 512, 128, 4, n).transpose(0, 1, 3, 2))
    if fmt == "e4m3":
        words = by_word.astype(ml_dtypes.float8_e4m3fn).view(np.uint8)
    else:
        c = by_word.astype(ml_dtypes.float4_e2m1fn).view(np.uint8) & 0xF
        words = (c[..., 0::2] | (c[..., 1::2] << 4)).reshape(k // 512, 128, 2 * n)
    return np.ascontiguousarray(words), np.ascontiguousarray(byte.astype(np.uint8).reshape(k // 512, 16, n))


def unpack_weight(words, scales, fmt):
    g, _, n = scales.shape
    words = np.ascontiguousarray(words).reshape(g, 128, n, -1)
    if fmt == "e4m3":
        vals = words.view(ml_dtypes.float8_e4m3fn).astype(np.float64)
    else:
        nib = np.empty((g, 128, n, 4), np.uint8)
        nib[..., 0::2] = words & 0xF
        nib[..., 1::2] = words >> 4
        vals = E2M1[nib]
    vals = vals * np.repeat(np.exp2(scales.astype(np.float64) - 127.0), 8, axis=1)[..., None]
    return vals.transpose(0, 1, 3, 2).reshape(g * 512, n)


K, T, J, R, N = 1024, 1024, 512, 512, 512


def setup_inputs():
    n = np.random.standard_normal
    idx = np.random.permutation(T)[:J]
    fk = mx_kscale(K)
    fr = mx_kscale(R)
    xtp = pack_weight(n((K, T)) * np.random.uniform(0.3, 1.9, (1, T)) / fk[:, None], "e4m3")
    wap = pack_weight(n((K, R)) * 1 / np.sqrt(K) * fk[:, None], "e2m1")
    wbp = pack_weight(n((R, N)) * 1 / np.sqrt(R) / fr[:, None], "e4m3")
    return {
        "xt_words": xtp[0],
        "xt_scales": xtp[1],
        "wa_words": wap[0],
        "wa_scales": wap[1],
        "fr": (np.random.uniform(0.5, 2.0, (R, 1)) * fr[:, None]).astype(np.float32),
        "wb_words": wbp[0],
        "wb_scales": wbp[1],
        "res": (1.0 * n((N, T))).astype(np.float32),
        "offs": striped(idx),
    }


def reference(xt_words, xt_scales, wa_words, wa_scales, fr, wb_words, wb_scales, res, offs):
    idx = unstriped(offs)
    xtu = unpack_weight(xt_words, xt_scales, "e4m3")
    wau = unpack_weight(wa_words, wa_scales, "e2m1")
    wbu = unpack_weight(wb_words, wb_scales, "e4m3")
    xtidxg = xtu[:, idx]
    z = xtidxg.T @ wau
    d = z - np.mean(z, axis=1, keepdims=True)
    e = d / np.sqrt(np.mean(np.square(d), axis=1, keepdims=True) + 0.01)
    et = e.T
    hid = et * f64(fr)
    hidq = mxq(hid, 0, "e4m3")
    p = wbu.T @ hidq
    pp = np.zeros((N, T))
    pp[:, idx] = p
    y = pp + 0.3 * f64(res)
    return y

@@ -1,0 +1,197 @@
+from contextlib import ExitStack
+
+import concourse.mybir as mybir
+from concourse.masks import make_identity
+
+K, T, J, R, N = 1024, 1024, 512, 512, 512
+FLOPS = 2 * J * K * R + 2 * J * R * N
+
+F32 = mybir.dt.float32
+BF16 = mybir.dt.bfloat16
+I32 = mybir.dt.int32
+U32 = mybir.dt.uint32
+U16 = mybir.dt.uint16
+U8 = mybir.dt.uint8
+FP8X4 = mybir.dt.float8_e4m3fn_x4
+FP4X4 = mybir.dt.float4_e2m1fn_x4
+ACT = mybir.ActivationFunctionType
+ALU = mybir.AluOpType
+
+P = 128
+PACK = 4
+PASSES = K // (P * PACK)
+CH = J // P
+NT = N // P
+EPS = 0.01
+RES_GAIN = 0.3
+
+
+def tile_moe_expert_hidden_rows_levelled_kernel(
+    tc, xt_words, xt_scales, wa_words, wa_scales, fr, wb_words, wb_scales, res, offs, out
+):
+    nc = tc.nc
+    with ExitStack() as ctx:
+        keep = ctx.enter_context(tc.tile_pool(name="keep", bufs=1))
+        psum = ctx.enter_context(tc.psum_pool(name="psum", bufs=1))
+
+        offsets = keep.tile([P, J // 16], U16, name="offsets")
+        xs = keep.tile([P, PASSES, T], U8, name="xs", align_bytes=64)
+        was = keep.tile([P, PASSES, R], U8, name="was", align_bytes=64)
+        wbs = keep.tile([P, 1, N], U8, name="wbs", align_bytes=64)
+        xw = [keep.tile([P, T], I32, name="xw%d" % z, align_bytes=64) for z in range(PASSES)]
+        waw = keep.tile([P, PASSES, 2 * R], U8, name="waw", align_bytes=64)
+        wbw = keep.tile([P, N], I32, name="wbw", align_bytes=64)
+        fr4 = keep.tile([P, PACK], F32, name="fr4")
+        rs = [keep.tile([P, T], F32, name="rs%d" % n) for n in range(NT)]
+        win = [keep.tile([P, T], F32, name="win%d" % n) for n in range(NT)]
+        ident = keep.tile([P, P], F32, name="ident")
+        warm = keep.tile([P, 2], F32, name="warm")
+
+        def load_plane(plane, src):
+            for q in range(4):
+                nc.sync.dma_start(
+                    plane[32 * q : 32 * q + 4].bitcast(I32),
+                    src[:, 4 * q : 4 * q + 4, :].rearrange("z q c -> q z c").bitcast(I32),
+                )
+
+        def zero_plane(plane):
+            nc.gpsimd.memset(plane[:].rearrange("p z c -> p (z c)").bitcast(I32), 0)
+
+        zero_plane(xs)
+        zero_plane(was)
+        nc.vector.memset(warm[:, 0:1], 1.0)
+        zero_plane(wbs)
+        nc.scalar.activation(warm[:, 1:2], warm[:, 0:1], ACT.Abs_reciprocal_sqrt)
+        make_identity(nc, ident[:])
+
+        nc.sync.dma_start(offsets[:], offs)
+        nc.sync.dma_start(fr4[:], fr.rearrange("(p t) o -> p (t o)", t=PACK))
+        nc.sync.dma_start(waw[:].bitcast(I32), wa_words.rearrange("z p c -> p z c").bitcast(I32))
+        load_plane(xs, xt_scales)
+        for z in range(PASSES):
+            nc.sync.dma_start(xw[z][:], xt_words[z].rearrange("p c r -> p (c r)").bitcast(I32))
+        load_plane(was, wa_scales)
+        nc.sync.dma_start(wbw[:], wb_words[0].rearrange("p c r -> p (c r)").bitcast(I32))
+        load_plane(wbs, wb_scales)
+        for n in range(NT):
+            nc.sync.dma_start(rs[n][:], res[n * P : (n + 1) * P, :])
+        for n in range(NT):
+            (nc.vector if n < 2 else nc.gpsimd).memset(win[n][:], 0.0)
+
+        def listed(j0, j1):
+            return offsets[:, j0 // 16 : j1 // 16]
+
+        sg = []
+        for z in range(PASSES):
+            s = keep.tile([P, J], U8, name="sg%d" % z, align_bytes=64)
+            nc.vector.tensor_copy(s[:], xs[:, z, :].indirect(offsets[:]))
+            sg.append(s)
+
+        codes = keep.tile([P, J], U32, name="codes", align_bytes=64)
+        hs = keep.tile([P, J], U8, name="hs", align_bytes=64)
+        pt = [keep.tile([P, J], F32, name="pt%d" % n) for n in range(NT)]
+
+        zs = [None] * CH
+
+        def products(c):
+            zp = psum.tile([P, R], F32, name="z%d" % c, tag="z%d" % c)
+            zs[c] = zp
+            for z in range(PASSES):
+                g = keep.tile([P, P], U32, name="xg%d_%d" % (z, c), tag="xg%d_%d" % (z, c % 3), align_bytes=64)
+                nc.vector.tensor_copy(g[:], xw[z][:].bitcast(U32).indirect(listed(c * P, (c + 1) * P)))
+                nc.tensor.matmul_mx(
+                    out=zp[:],
+                    lhsT=g[:].bitcast(FP8X4),
+                    lhsT_scale=sg[z][:, c * P : (c + 1) * P],
+                    rhs=waw[:, z, :].bitcast(FP4X4),
+                    rhs_scale=was[:, z, :],
+                    start=(z == 0),
+                    stop=(z == PASSES - 1),
+                )
+
+        es = [None] * CH
+
+        def level(c):
+            zp = zs[c]
+            bn = keep.tile([P, 6], F32, name="bn%d" % c)
+            mv = keep.tile([P, 2], F32, name="mv%d" % c)
+            st = keep.tile([P, 4], F32, name="st%d" % c)
+            e = keep.tile([P, PACK, P], F32, name="e%d" % c, tag="e%d" % c)
+            es[c] = e
+            nc.vector.bn_stats(bn[:], zp[:])
+            nc.vector.bn_aggr(mv[:], bn[:])
+            nc.scalar.activation(st[:, 0:1], mv[:, 1:2], ACT.Abs_reciprocal_sqrt, bias=EPS)
+            nc.scalar.mul(st[:, 1:2], mv[:, 0:1], -1.0)
+            nc.scalar.activation(st[:, 2:3], st[:, 1:2], ACT.Identity, scale=st[:, 0:1])
+            nc.scalar.activation(
+                e[:], zp[:].rearrange("p (m t) -> p t m", t=PACK), ACT.Identity, scale=st[:, 0:1], bias=st[:, 2:3]
+            )
+
+        def turn(c):
+            e = es[c]
+            tp = psum.tile([P, PACK, P], F32, name="tp%d" % c, tag="tp%d" % (c % 2))
+            for t in range(PACK):
+                nc.tensor.transpose(tp[:, t, :], e[:, t, :], ident[:])
+            hid = keep.tile([P, P, PACK], BF16, name="hid%d" % c, align_bytes=64)
+            nc.vector.tensor_tensor(
+                hid[:], tp[:].rearrange("p t j -> p j t"), fr4[:].unsqueeze(1).to_broadcast([P, P, PACK]), ALU.mult
+            )
+            cols = slice(c * P, (c + 1) * P)
+            nc.vector.quantize_mx(
+                out=codes[:, cols].bitcast(FP8X4), scales=hs[:, cols], in_=hid[:].rearrange("p j t -> p (j t)")
+            )
+
+        def second_layer(tag, pieces):
+            bank = psum.tile([P, R], F32, name="p_" + tag, tag=tag)
+            at = 0
+            spans = []
+            for n, j0, j1 in pieces:
+                a = at
+                for m0, m1 in ((j0, j1),) if j1 - j0 != 3 * P else ((j0, j0 + 2 * P), (j0 + 2 * P, j1)):
+                    nc.tensor.matmul_mx(
+                        out=bank[:, at : at + m1 - m0],
+                        lhsT=wbw[:, n * P : (n + 1) * P].bitcast(FP8X4),
+                        lhsT_scale=wbs[:, 0, n * P : (n + 1) * P],
+                        rhs=codes[:, m0:m1].bitcast(FP8X4),
+                        rhs_scale=hs[:, m0:m1],
+                        start=True,
+                        stop=True,
+                    )
+                    at = at + m1 - m0
+                spans.append((n, j0, j1, a))
+            for n, j0, j1, a in spans:
+                nc.scalar.copy(pt[n][:, j0:j1], bank[:, a : a + j1 - j0])
+                nc.vector.tensor_copy(win[n][:].indirect(listed(j0, j1)), pt[n][:, j0:j1])
+
+        def finish(n):
+            rows = slice(n * P, (n + 1) * P)
+            o = keep.tile([P, T], F32, name="o%d" % n)
+            if n < NT - 1:
+                scaled = keep.tile([P, T], F32, name="scaled%d" % n, tag=("e2", "e3", "e2")[n])
+                for h in range(2):
+                    half = slice(h * T // 2, (h + 1) * T // 2)
+                    nc.scalar.mul(scaled[:, half], rs[n][:, half], RES_GAIN)
+                nc.gpsimd.tensor_tensor(o[:], win[n][:], scaled[:], ALU.add)
+                nc.sync.dma_start(out[rows, :], o[:])
+            else:
+                for h in range(2):
+                    half = slice(h * T // 2, (h + 1) * T // 2)
+                    nc.vector.scalar_tensor_tensor(
+                        o[:, half], rs[n][:, half], RES_GAIN, win[n][:, half], ALU.mult, ALU.add
+                    )
+                    (nc.sync, nc.scalar)[h].dma_start(out[rows, half], o[:, half])
+
+        for c in range(CH - 1):
+            products(c)
+        level(0)
+        products(CH - 1)
+        for c in range(1, CH):
+            level(c)
+        for c in range(CH):
+            turn(c)
+        second_layer("pa", [(0, 0, 3 * P)])
+        second_layer("pb", [(0, 3 * P, J)])
+        finish(0)
+        for n in range(1, NT):
+            second_layer("z%d" % n, [(n, 0, J)])
+            finish(n)

@@ -38,7 +38,7 @@ def tile_moe_expert_hidden_rows_levelled_kernel(
         xs = keep.tile([P, PASSES, T], U8, name="xs", align_bytes=64)
         was = keep.tile([P, PASSES, R], U8, name="was", align_bytes=64)
         wbs = keep.tile([P, 1, N], U8, name="wbs", align_bytes=64)
-        xw = [keep.tile([P, T], I32, name="xw%d" % z, align_bytes=64) for z in range(PASSES)]
+        xw = keep.tile([P, PASSES, T], I32, name="xw", align_bytes=64)
         waw = keep.tile([P, PASSES, 2 * R], U8, name="waw", align_bytes=64)
         wbw = keep.tile([P, N], I32, name="wbw", align_bytes=64)
         fr4 = keep.tile([P, PACK], F32, name="fr4")
@@ -66,10 +66,9 @@ def tile_moe_expert_hidden_rows_levelled_kernel(
 
         nc.sync.dma_start(offsets[:], offs)
         nc.sync.dma_start(fr4[:], fr.rearrange("(p t) o -> p (t o)", t=PACK))
-        nc.sync.dma_start(waw[:].bitcast(I32), wa_words.rearrange("z p c -> p z c").bitcast(I32))
         load_plane(xs, xt_scales)
-        for z in range(PASSES):
-            nc.sync.dma_start(xw[z][:], xt_words[z].rearrange("p c r -> p (c r)").bitcast(I32))
+        nc.sync.dma_start(waw[:].bitcast(I32), wa_words.rearrange("z p c -> p z c").bitcast(I32))
+        nc.sync.dma_start(xw[:], xt_words.rearrange("z p c r -> p z (c r)").bitcast(I32))
         load_plane(was, wa_scales)
         nc.sync.dma_start(wbw[:], wb_words[0].rearrange("p c r -> p (c r)").bitcast(I32))
         load_plane(wbs, wb_scales)
@@ -81,15 +80,20 @@ def tile_moe_expert_hidden_rows_levelled_kernel(
         def listed(j0, j1):
             return offsets[:, j0 // 16 : j1 // 16]
 
-        sg = []
-        for z in range(PASSES):
-            s = keep.tile([P, J], U8, name="sg%d" % z, align_bytes=64)
-            nc.vector.tensor_copy(s[:], xs[:, z, :].indirect(offsets[:]))
-            sg.append(s)
+        sg = [keep.tile([P, J], U8, name="sg%d" % z, align_bytes=64) for z in range(PASSES)]
+        xg = [keep.tile([P, J], U32, name="xg%d" % z, align_bytes=64) for z in range(PASSES)]
 
-        codes = keep.tile([P, J], U32, name="codes", align_bytes=64)
-        hs = keep.tile([P, J], U8, name="hs", align_bytes=64)
-        pt = [keep.tile([P, J], F32, name="pt%d" % n) for n in range(NT)]
+        def gather_scales(j0, j1):
+            for z in range(PASSES):
+                nc.vector.tensor_copy(sg[z][:, j0:j1], xs[:, z, :].indirect(listed(j0, j1)))
+
+        def gather_words(j0, j1):
+            for z in range(PASSES):
+                nc.vector.tensor_copy(xg[z][:, j0:j1], xw[:, z, :].bitcast(U32).indirect(listed(j0, j1)))
+
+        codes = keep.tile([P, J], U32, name="codes", tag="codes", align_bytes=64)
+        hs = keep.tile([P, J], U8, name="hs", tag="late", align_bytes=64)
+
 
         zs = [None] * CH
 
@@ -97,11 +101,9 @@ def tile_moe_expert_hidden_rows_levelled_kernel(
             zp = psum.tile([P, R], F32, name="z%d" % c, tag="z%d" % c)
             zs[c] = zp
             for z in range(PASSES):
-                g = keep.tile([P, P], U32, name="xg%d_%d" % (z, c), tag="xg%d_%d" % (z, c % 3), align_bytes=64)
-                nc.vector.tensor_copy(g[:], xw[z][:].bitcast(U32).indirect(listed(c * P, (c + 1) * P)))
                 nc.tensor.matmul_mx(
                     out=zp[:],
-                    lhsT=g[:].bitcast(FP8X4),
+                    lhsT=xg[z][:, c * P : (c + 1) * P].bitcast(FP8X4),
                     lhsT_scale=sg[z][:, c * P : (c + 1) * P],
                     rhs=waw[:, z, :].bitcast(FP4X4),
                     rhs_scale=was[:, z, :],
@@ -111,63 +113,63 @@ def tile_moe_expert_hidden_rows_levelled_kernel(
 
         es = [None] * CH
 
+        frb = keep.tile([P, R], F32, name="frb")
+        spread = psum.tile([P, PACK, P], F32, name="spread", tag="pa")
+        for t in range(PACK):
+            nc.tensor.transpose(spread[:, t, :], fr4[:, t : t + 1].to_broadcast([P, P]), ident[:])
+        nc.scalar.copy(frb[:].rearrange("p (m t) -> p m t", t=PACK), spread[:].rearrange("p t m -> p m t"))
+
         def level(c):
             zp = zs[c]
             bn = keep.tile([P, 6], F32, name="bn%d" % c)
             mv = keep.tile([P, 2], F32, name="mv%d" % c)
-            st = keep.tile([P, 4], F32, name="st%d" % c)
-            e = keep.tile([P, PACK, P], F32, name="e%d" % c, tag="e%d" % c)
-            es[c] = e
+            rstd = keep.tile([P, 1], F32, name="rstd%d" % c)
+            d = keep.tile([P, R], F32, name="d%d" % c, tag="d%d" % c, align_bytes=64)
+            h = keep.tile([P, 2, P, 2], BF16, name="h%d" % c, tag="h%d" % c, align_bytes=64)
+            es[c] = h
             nc.vector.bn_stats(bn[:], zp[:])
             nc.vector.bn_aggr(mv[:], bn[:])
-            nc.scalar.activation(st[:, 0:1], mv[:, 1:2], ACT.Abs_reciprocal_sqrt, bias=EPS)
-            nc.scalar.mul(st[:, 1:2], mv[:, 0:1], -1.0)
-            nc.scalar.activation(st[:, 2:3], st[:, 1:2], ACT.Identity, scale=st[:, 0:1])
+            nc.vector.scalar_tensor_tensor(d[:], zp[:], mv[:, 0:1], frb[:], ALU.subtract, ALU.mult)
+            nc.scalar.activation(rstd[:], mv[:, 1:2], ACT.Abs_reciprocal_sqrt, bias=EPS)
             nc.scalar.activation(
-                e[:], zp[:].rearrange("p (m t) -> p t m", t=PACK), ACT.Identity, scale=st[:, 0:1], bias=st[:, 2:3]
+                h[:], d[:].rearrange("p (m u s) -> p u m s", u=2, s=2), ACT.Identity, scale=rstd[:]
             )
 
         def turn(c):
-            e = es[c]
-            tp = psum.tile([P, PACK, P], F32, name="tp%d" % c, tag="tp%d" % (c % 2))
-            for t in range(PACK):
-                nc.tensor.transpose(tp[:, t, :], e[:, t, :], ident[:])
-            hid = keep.tile([P, P, PACK], BF16, name="hid%d" % c, align_bytes=64)
-            nc.vector.tensor_tensor(
-                hid[:], tp[:].rearrange("p t j -> p j t"), fr4[:].unsqueeze(1).to_broadcast([P, P, PACK]), ALU.mult
-            )
+            words = es[c][:].rearrange("p u m s -> p u (m s)").bitcast(F32)
+            tp = psum.tile([P, 2, P], F32, name="tp%d" % c, tag="tp%d" % (c % 2))
+            for u in range(2):
+                nc.tensor.transpose(tp[:, u, :], words[:, u, :], ident[:])
+            hid = keep.tile([P, P, PACK], BF16, name="hid%d" % c, tag="hid%d" % c, align_bytes=64)
+            nc.scalar.copy(hid[:].bitcast(F32), tp[:].rearrange("p u j -> p j u"))
             cols = slice(c * P, (c + 1) * P)
             nc.vector.quantize_mx(
                 out=codes[:, cols].bitcast(FP8X4), scales=hs[:, cols], in_=hid[:].rearrange("p j t -> p (j t)")
             )
 
-        def second_layer(tag, pieces):
-            bank = psum.tile([P, R], F32, name="p_" + tag, tag=tag)
-            at = 0
-            spans = []
-            for n, j0, j1 in pieces:
-                a = at
-                for m0, m1 in ((j0, j1),) if j1 - j0 != 3 * P else ((j0, j0 + 2 * P), (j0 + 2 * P, j1)):
-                    nc.tensor.matmul_mx(
-                        out=bank[:, at : at + m1 - m0],
-                        lhsT=wbw[:, n * P : (n + 1) * P].bitcast(FP8X4),
-                        lhsT_scale=wbs[:, 0, n * P : (n + 1) * P],
-                        rhs=codes[:, m0:m1].bitcast(FP8X4),
-                        rhs_scale=hs[:, m0:m1],
-                        start=True,
-                        stop=True,
-                    )
-                    at = at + m1 - m0
-                spans.append((n, j0, j1, a))
-            for n, j0, j1, a in spans:
-                nc.scalar.copy(pt[n][:, j0:j1], bank[:, a : a + j1 - j0])
-                nc.vector.tensor_copy(win[n][:].indirect(listed(j0, j1)), pt[n][:, j0:j1])
+        def second_layer(tag, slot, ns, j0, j1):
+            w = j1 - j0
+            bank = psum.tile([P, len(ns), w], F32, name="p_" + tag, tag=tag)
+            for i, n in enumerate(ns):
+                nc.tensor.matmul_mx(
+                    out=bank[:, i, :],
+                    lhsT=wbw[:, n * P : (n + 1) * P].bitcast(FP8X4),
+                    lhsT_scale=wbs[:, 0, n * P : (n + 1) * P],
+                    rhs=codes[:, j0:j1].bitcast(FP8X4),
+                    rhs_scale=hs[:, j0:j1],
+                    start=True,
+                    stop=True,
+                )
+            pt = keep.tile([P, len(ns), w], F32, name="pt_" + slot, tag=slot, align_bytes=64)
+            nc.scalar.copy(pt[:], bank[:])
+            for i, n in enumerate(ns):
+                nc.vector.tensor_copy(win[n][:].indirect(listed(j0, j1)), pt[:, i, :])
 
         def finish(n):
             rows = slice(n * P, (n + 1) * P)
             o = keep.tile([P, T], F32, name="o%d" % n)
             if n < NT - 1:
-                scaled = keep.tile([P, T], F32, name="scaled%d" % n, tag=("e2", "e3", "e2")[n])
+                scaled = keep.tile([P, T], F32, name="scaled%d" % n, tag=("d3", "hid2", "pl")[n], align_bytes=64)
                 for h in range(2):
                     half = slice(h * T // 2, (h + 1) * T // 2)
                     nc.scalar.mul(scaled[:, half], rs[n][:, half], RES_GAIN)
@@ -179,19 +181,31 @@ def tile_moe_expert_hidden_rows_levelled_kernel(
                     nc.vector.scalar_tensor_tensor(
                         o[:, half], rs[n][:, half], RES_GAIN, win[n][:, half], ALU.mult, ALU.add
                     )
-                    (nc.sync, nc.scalar)[h].dma_start(out[rows, half], o[:, half])
+                    nc.scalar.dma_start(out[rows, half], o[:, half])
 
-        for c in range(CH - 1):
-            products(c)
+        gather_scales(0, J)
+        gather_words(0, P)
+        products(0)
+        gather_words(P, 2 * P)
+        products(1)
+        gather_words(2 * P, J)
+        products(2)
+        products(3)
         level(0)
-        products(CH - 1)
-        for c in range(1, CH):
-            level(c)
-        for c in range(CH):
-            turn(c)
-        second_layer("pa", [(0, 0, 3 * P)])
-        second_layer("pb", [(0, 3 * P, J)])
+        turn(0)
+        level(1)
+        turn(1)
+        second_layer("pa", "h1", [0, 1], 0, P)
+        level(2)
+        turn(2)
+        second_layer("pb", "h2", [0, 1], P, 2 * P)
+        level(3)
+        turn(3)
+        second_layer("z0", "h3", [0, 1], 2 * P, 3 * P)
+        second_layer("z1", "pl", [0, 1], 3 * P, J)
         finish(0)
-        for n in range(1, NT):
-            second_layer("z%d" % n, [(n, 0, J)])
-            finish(n)
+        finish(1)
+        second_layer("z2", "p2", [2], 0, J)
+        finish(2)
+        second_layer("z3", "p3", [3], 0, J)
+        finish(3)

from contextlib import ExitStack

import concourse.mybir as mybir
from concourse.masks import make_identity

K, T, J, R, N = 1024, 1024, 512, 512, 512
FLOPS = 2 * J * K * R + 2 * J * R * N

F32 = mybir.dt.float32
BF16 = mybir.dt.bfloat16
I32 = mybir.dt.int32
U32 = mybir.dt.uint32
U16 = mybir.dt.uint16
U8 = mybir.dt.uint8
FP8X4 = mybir.dt.float8_e4m3fn_x4
FP4X4 = mybir.dt.float4_e2m1fn_x4
ACT = mybir.ActivationFunctionType
ALU = mybir.AluOpType

P = 128
PACK = 4
PASSES = K // (P * PACK)
CH = J // P
NT = N // P
EPS = 0.01
RES_GAIN = 0.3


def tile_moe_expert_hidden_rows_levelled_kernel(
    tc, xt_words, xt_scales, wa_words, wa_scales, fr, wb_words, wb_scales, res, offs, out
):
    nc = tc.nc
    with ExitStack() as ctx:
        keep = ctx.enter_context(tc.tile_pool(name="keep", bufs=1))
        psum = ctx.enter_context(tc.psum_pool(name="psum", bufs=1))

        offsets = keep.tile([P, J // 16], U16, name="offsets")
        xs = keep.tile([P, PASSES, T], U8, name="xs", align_bytes=64)
        was = keep.tile([P, PASSES, R], U8, name="was", align_bytes=64)
        wbs = keep.tile([P, 1, N], U8, name="wbs", align_bytes=64)
        xw = keep.tile([P, PASSES, T], I32, name="xw", align_bytes=64)
        waw = keep.tile([P, PASSES, 2 * R], U8, name="waw", align_bytes=64)
        wbw = keep.tile([P, N], I32, name="wbw", align_bytes=64)
        fr4 = keep.tile([P, PACK], F32, name="fr4")
        rs = [keep.tile([P, T], F32, name="rs%d" % n) for n in range(NT)]
        win = [keep.tile([P, T], F32, name="win%d" % n) for n in range(NT)]
        ident = keep.tile([P, P], F32, name="ident")
        warm = keep.tile([P, 2], F32, name="warm")

        def load_plane(plane, src):
            for q in range(4):
                nc.sync.dma_start(
                    plane[32 * q : 32 * q + 4].bitcast(I32),
                    src[:, 4 * q : 4 * q + 4, :].rearrange("z q c -> q z c").bitcast(I32),
                )

        def zero_plane(plane):
            nc.gpsimd.memset(plane[:].rearrange("p z c -> p (z c)").bitcast(I32), 0)

        zero_plane(xs)
        zero_plane(was)
        nc.vector.memset(warm[:, 0:1], 1.0)
        zero_plane(wbs)
        nc.scalar.activation(warm[:, 1:2], warm[:, 0:1], ACT.Abs_reciprocal_sqrt)
        make_identity(nc, ident[:])

        nc.sync.dma_start(offsets[:], offs)
        nc.sync.dma_start(fr4[:], fr.rearrange("(p t) o -> p (t o)", t=PACK))
        load_plane(xs, xt_scales)
        nc.sync.dma_start(waw[:].bitcast(I32), wa_words.rearrange("z p c -> p z c").bitcast(I32))
        nc.sync.dma_start(xw[:], xt_words.rearrange("z p c r -> p z (c r)").bitcast(I32))
        load_plane(was, wa_scales)
        nc.sync.dma_start(wbw[:], wb_words[0].rearrange("p c r -> p (c r)").bitcast(I32))
        load_plane(wbs, wb_scales)
        for n in range(NT):
            nc.sync.dma_start(rs[n][:], res[n * P : (n + 1) * P, :])
        for n in range(NT):
            (nc.vector if n < 2 else nc.gpsimd).memset(win[n][:], 0.0)

        def listed(j0, j1):
            return offsets[:, j0 // 16 : j1 // 16]

        sg = [keep.tile([P, J], U8, name="sg%d" % z, align_bytes=64) for z in range(PASSES)]
        xg = [keep.tile([P, J], U32, name="xg%d" % z, align_bytes=64) for z in range(PASSES)]

        def gather_scales(j0, j1):
            for z in range(PASSES):
                nc.vector.tensor_copy(sg[z][:, j0:j1], xs[:, z, :].indirect(listed(j0, j1)))

        def gather_words(j0, j1):
            for z in range(PASSES):
                nc.vector.tensor_copy(xg[z][:, j0:j1], xw[:, z, :].bitcast(U32).indirect(listed(j0, j1)))

        codes = keep.tile([P, J], U32, name="codes", tag="codes", align_bytes=64)
        hs = keep.tile([P, J], U8, name="hs", tag="late", align_bytes=64)


        zs = [None] * CH

        def products(c):
            zp = psum.tile([P, R], F32, name="z%d" % c, tag="z%d" % c)
            zs[c] = zp
            for z in range(PASSES):
                nc.tensor.matmul_mx(
                    out=zp[:],
                    lhsT=xg[z][:, c * P : (c + 1) * P].bitcast(FP8X4),
                    lhsT_scale=sg[z][:, c * P : (c + 1) * P],
                    rhs=waw[:, z, :].bitcast(FP4X4),
                    rhs_scale=was[:, z, :],
                    start=(z == 0),
                    stop=(z == PASSES - 1),
                )

        es = [None] * CH

        frb = keep.tile([P, R], F32, name="frb")
        spread = psum.tile([P, PACK, P], F32, name="spread", tag="pa")
        for t in range(PACK):
            nc.tensor.transpose(spread[:, t, :], fr4[:, t : t + 1].to_broadcast([P, P]), ident[:])
        nc.scalar.copy(frb[:].rearrange("p (m t) -> p m t", t=PACK), spread[:].rearrange("p t m -> p m t"))

        def level(c):
            zp = zs[c]
            bn = keep.tile([P, 6], F32, name="bn%d" % c)
            mv = keep.tile([P, 2], F32, name="mv%d" % c)
            rstd = keep.tile([P, 1], F32, name="rstd%d" % c)
            d = keep.tile([P, R], F32, name="d%d" % c, tag="d%d" % c, align_bytes=64)
            h = keep.tile([P, 2, P, 2], BF16, name="h%d" % c, tag="h%d" % c, align_bytes=64)
            es[c] = h
            nc.vector.bn_stats(bn[:], zp[:])
            nc.vector.bn_aggr(mv[:], bn[:])
            nc.vector.scalar_tensor_tensor(d[:], zp[:], mv[:, 0:1], frb[:], ALU.subtract, ALU.mult)
            nc.scalar.activation(rstd[:], mv[:, 1:2], ACT.Abs_reciprocal_sqrt, bias=EPS)
            nc.scalar.activation(
                h[:], d[:].rearrange("p (m u s) -> p u m s", u=2, s=2), ACT.Identity, scale=rstd[:]
            )

        def turn(c):
            words = es[c][:].rearrange("p u m s -> p u (m s)").bitcast(F32)
            tp = psum.tile([P, 2, P], F32, name="tp%d" % c, tag="tp%d" % (c % 2))
            for u in range(2):
                nc.tensor.transpose(tp[:, u, :], words[:, u, :], ident[:])
            hid = keep.tile([P, P, PACK], BF16, name="hid%d" % c, tag="hid%d" % c, align_bytes=64)
            nc.scalar.copy(hid[:].bitcast(F32), tp[:].rearrange("p u j -> p j u"))
            cols = slice(c * P, (c + 1) * P)
            nc.vector.quantize_mx(
                out=codes[:, cols].bitcast(FP8X4), scales=hs[:, cols], in_=hid[:].rearrange("p j t -> p (j t)")
            )

        def second_layer(tag, slot, ns, j0, j1):
            w = j1 - j0
            bank = psum.tile([P, len(ns), w], F32, name="p_" + tag, tag=tag)
            for i, n in enumerate(ns):
                nc.tensor.matmul_mx(
                    out=bank[:, i, :],
                    lhsT=wbw[:, n * P : (n + 1) * P].bitcast(FP8X4),
                    lhsT_scale=wbs[:, 0, n * P : (n + 1) * P],
                    rhs=codes[:, j0:j1].bitcast(FP8X4),
                    rhs_scale=hs[:, j0:j1],
                    start=True,
                    stop=True,
                )
            pt = keep.tile([P, len(ns), w], F32, name="pt_" + slot, tag=slot, align_bytes=64)
            nc.scalar.copy(pt[:], bank[:])
            for i, n in enumerate(ns):
                nc.vector.tensor_copy(win[n][:].indirect(listed(j0, j1)), pt[:, i, :])

        def finish(n):
            rows = slice(n * P, (n + 1) * P)
            o = keep.tile([P, T], F32, name="o%d" % n)
            if n < NT - 1:
                scaled = keep.tile([P, T], F32, name="scaled%d" % n, tag=("d3", "hid2", "pl")[n], align_bytes=64)
                for h in range(2):
                    half = slice(h * T // 2, (h + 1) * T // 2)
                    nc.scalar.mul(scaled[:, half], rs[n][:, half], RES_GAIN)
                nc.gpsimd.tensor_tensor(o[:], win[n][:], scaled[:], ALU.add)
                nc.sync.dma_start(out[rows, :], o[:])
            else:
                for h in range(2):
                    half = slice(h * T // 2, (h + 1) * T // 2)
                    nc.vector.scalar_tensor_tensor(
                        o[:, half], rs[n][:, half], RES_GAIN, win[n][:, half], ALU.mult, ALU.add
                    )
                    nc.scalar.dma_start(out[rows, half], o[:, half])

        gather_scales(0, J)
        gather_words(0, P)
        products(0)
        gather_words(P, 2 * P)
        products(1)
        gather_words(2 * P, J)
        products(2)
        products(3)
        level(0)
        turn(0)
        level(1)
        turn(1)
        second_layer("pa", "h1", [0, 1], 0, P)
        level(2)
        turn(2)
        second_layer("pb", "h2", [0, 1], P, 2 * P)
        level(3)
        turn(3)
        second_layer("z0", "h3", [0, 1], 2 * P, 3 * P)
        second_layer("z1", "pl", [0, 1], 3 * P, J)
        finish(0)
        finish(1)
        second_layer("z2", "p2", [2], 0, J)
        finish(2)
        second_layer("z3", "p3", [3], 0, J)
        finish(3)
